import numpy as np
import ml_dtypes


def mxq(x, axis, fmt="e4m3"):
    dtype, down = {"e4m3": (ml_dtypes.float8_e4m3fn, 7), "e5m2": (ml_dtypes.float8_e5m2, 14)}[fmt]
    v = np.moveaxis(np.asarray(x, np.float32).astype(ml_dtypes.bfloat16).astype(np.float64), axis, -1)
    blocks = v.reshape(v.shape[:-1] + (-1, 32))
    amax = np.abs(blocks).max(-1, keepdims=True)
    byte = np.maximum(np.where(amax > 0, np.frexp(amax)[1] - 1 + 127, 0) - down, 1)
    scale = np.exp2(byte - 127.0)
    codes = (blocks / scale).astype(np.float32).astype(dtype).astype(np.float64)
    return np.moveaxis((codes * scale).reshape(v.shape), -1, axis)


WIDE = False


def mx_kscale(k):
    if not WIDE:
        return np.ones(k)
    levels = np.array([10, -10, 5, -5, 0])
    if k % 512:
        return np.exp2(np.random.permutation(np.resize(levels, k // 32))).repeat(32)
    a = np.empty((k // 512, 16))
    for p in range(k // 512):
        a[p, :8] = np.random.permutation(np.resize(levels, 8))
        for g in range(8):
            far = levels[np.abs(levels - a[p, g]) >= 10]
            a[p, g + 8] = far[np.random.randint(len(far))]
    return np.exp2(a.ravel()).repeat(32)


def f64(x):
    return np.asarray(x).astype(np.float64)


def striped(idx):
    return np.tile(idx.reshape(-1, 16).T, (8, 1)).astype(np.uint16)


def unstriped(offs):
    return offs[:16].T.reshape(-1).astype(np.int64)


def striped8(idx):
    return np.concatenate([x.reshape(-1, 16).T for x in idx]).astype(np.uint16)


def runs(offs, k):
    lists = np.stack([offs[16 * r : 16 * r + 16].T.reshape(-1) for r in range(8)]).astype(np.int64)
    return lists[np.arange(k) % 512 // 64]


def pack_weight(w):
    k, n = w.shape
    w = f64(np.asarray(w, np.float32).astype(ml_dtypes.bfloat16)).reshape(k // 32, 32, n)
    amax = np.abs(w).max(1)
    byte = np.clip(np.where(amax > 0, np.frexp(amax)[1] - 1 + 127 - 7, 1), 1, 254)
    scaled = (w * np.exp2(127.0 - byte)[:, None, :]).reshape(k, n).astype(np.float32)
    words = np.ascontiguousarray(scaled.reshape(k // 512, 128, 4, n).transpose(0, 1, 3, 2)).astype(ml_dtypes.float8_e4m3fn).view(np.uint8)
    return words, np.ascontiguousarray(byte.astype(np.uint8).reshape(k // 512, 16, n))


def unpack_weight(words, scales):
    g, p, n, _ = words.shape
    vals = np.ascontiguousarray(words).view(ml_dtypes.float8_e4m3fn).astype(np.float64) * np.repeat(np.exp2(scales.astype(np.float64) - 127.0), 8, axis=1)[..., None]
    return vals.transpose(0, 1, 3, 2).reshape(g * 512, n)


E2M1 = np.array([0.0, 0.5, 1.0, 1.5, 2.0, 3.0, 4.0, 6.0, -0.0, -0.5, -1.0, -1.5, -2.0, -3.0, -4.0, -6.0])


def pack_fp4(w):
    k, n = w.shape
    w = f64(np.asarray(w, np.float32).astype(ml_dtypes.bfloat16)).reshape(k // 32, 32, n)
    amax = np.abs(w).max(1)
    mant, ex = np.frexp(amax / 6.0)
    byte = np.clip(np.where(amax > 0, np.where(mant > 0.5, ex, ex - 1) + 127, 1), 1, 254)
    scaled = (w * np.exp2(127.0 - byte)[:, None, :]).reshape(k, n).astype(np.float32)
    c = np.ascontiguousarray(scaled.reshape(k // 512, 128, 4, n).transpose(0, 1, 3, 2)).astype(ml_dtypes.float4_e2m1fn).view(np.uint8) & 0xF
    words = (c[..., 0::2] | (c[..., 1::2] << 4)).reshape(k // 512, 128, 2 * n)
    return np.ascontiguousarray(words), np.ascontiguousarray(byte.astype(np.uint8).reshape(k // 512, 16, n))


def unpack_fp4(words, scales):
    g, _, n = scales.shape
    words = np.ascontiguousarray(words).reshape(g, 128, n, 2)
    nib = np.empty((g, 128, n, 4), np.uint8)
    nib[..., 0::2] = words & 0xF
    nib[..., 1::2] = words >> 4
    vals = E2M1[nib] * np.repeat(np.exp2(scales.astype(np.float64) - 127.0), 8, axis=1)[..., None]
    return vals.transpose(0, 1, 3, 2).reshape(g * 512, n)


def sigmoid(v):
    return 1.0 / (1.0 + np.exp(-np.maximum(v, -700.0)))


K, T, S, H, C = 512, 2048, 512, 512, 512


def setup_inputs():
    n = np.random.standard_normal
    s = mx_kscale(K)[:, None]
    packed_xT = pack_weight(n((K, T)) * s)
    packed_w1 = pack_fp4(n((K, H)) / np.sqrt(2 * K) / s)
    packed_w2 = pack_fp4(n((K, H)) / np.sqrt(2 * K) / s)
    return {
        "x_words": packed_xT[0],
        "x_scales": packed_xT[1],
        "w1_words": packed_w1[0],
        "w1_scales": packed_w1[1],
        "w2_words": packed_w2[0],
        "w2_scales": packed_w2[1],
        "gs": (np.random.uniform(0.5, 1.5, (K, 1)) / s).astype(np.float32),
        "sl": np.random.uniform(1.0, 2.0, (C, 1)).astype(np.float32),
        "th": (0.5 * n((C, 1))).astype(np.float32),
        "offs": striped(np.random.permutation(T)[:S]),
        "hz": striped8(np.random.randint(0, T, (8, S))),
        "n1": striped8(np.stack([np.random.permutation(S) for _ in range(8)])),
        "n2": striped8(np.stack([np.random.permutation(S) for _ in range(8)])),
        "cand": striped(np.random.permutation(T)[:C]),
        "n3": striped8(np.stack([np.random.permutation(S) for _ in range(8)])),
        "n4": striped8(np.stack([np.random.permutation(S) for _ in range(8)])),
    }


def reference(x_words, x_scales, w1_words, w1_scales, w2_words, w2_scales, gs, sl, th, offs, hz, n1, n2, cand, n3, n4):
    x_cand = unpack_weight(x_words, x_scales)[:, unstriped(cand)]
    xq = unpack_weight(x_words, x_scales)[:, unstriped(offs)]
    x_hz = unpack_weight(x_words, x_scales)[np.arange(K)[:, None], runs(hz, K)]
    y = unpack_fp4(w1_words, w1_scales).T @ xq + unpack_fp4(w2_words, w2_scales).T @ x_hz
    ds = np.zeros((H, S))
    ds[np.arange(H)[:, None], runs(n1, H)] = y
    ds2 = np.zeros((H, S))
    ds2[np.arange(H)[:, None], runs(n2, H)] = y
    z = f64(gs) * np.maximum(ds, ds2)
    s = 0.0625 * ((x_cand.T @ mxq(z, 0, "e4m3")))
    sg = sigmoid(f64(sl) * (s[np.arange(C)[:, None], runs(n3, C)] - f64(th)))
    st = s * sg
    return st - (0.5 * (st[np.arange(C)[:, None], runs(n4, C)]))

@@ -1,0 +1,206 @@
+from contextlib import ExitStack
+
+import concourse.mybir as mybir
+
+K, T, S, H, C = 512, 2048, 512, 512, 512
+FLOPS = 3 * 2 * K * H * S
+
+F32 = mybir.dt.float32
+BF16 = mybir.dt.bfloat16
+I32 = mybir.dt.int32
+U32 = mybir.dt.uint32
+U16 = mybir.dt.uint16
+U8 = mybir.dt.uint8
+FP8X4 = mybir.dt.float8_e4m3fn_x4
+FP4X4 = mybir.dt.float4_e2m1fn_x4
+ALU = mybir.AluOpType
+ACT = mybir.ActivationFunctionType
+
+P = 128
+PACK = 4
+HALF = S // 2
+LIST_COLS = S // 16
+
+
+def tile_picked_thcsendtwoehp_none_p_kernel(
+    tc, x_words, x_scales, w1_words, w1_scales, w2_words, w2_scales, gs, sl, th, offs, hz, n1, n2, cand, n3, n4, out
+):
+    nc = tc.nc
+    with ExitStack() as ctx:
+        keep = ctx.enter_context(tc.tile_pool(name="keep", bufs=1))
+        psum = ctx.enter_context(tc.psum_pool(name="psum", bufs=1))
+
+        def load_list(name, src):
+            tile = keep.tile([P, LIST_COLS], U16, name=name)
+            nc.sync.dma_start(tile[:], src)
+            return tile
+
+        def load_rows(name, src, tag):
+            tile = keep.tile([P, PACK], F32, name=name, tag=tag, align_bytes=64)
+            nc.sync.dma_start(tile[:], src.rearrange("(p t) o -> p (t o)", t=PACK))
+            return tile
+
+        xs_table = keep.tile([P, T], U8, tag="bytes_then_words", align_bytes=64)
+        ws_raw = keep.tile([P, 2 * H], U8, align_bytes=64)
+        nc.gpsimd.memset(xs_table[:].bitcast(I32), 0)
+        nc.vector.memset(ws_raw[:].bitcast(I32), 0)
+
+        hz_list = load_list("hz_list", hz)
+        xs_rows = x_scales[0].bitcast(I32)
+        for r in range(4):
+            part_step, row_step = (16, 2) if r < 2 else (32, 4)
+            nc.scalar.dma_start(xs_table[r:P:part_step, :].bitcast(I32), xs_rows[r:16:row_step, :])
+        xw_table = keep.tile([P, T], I32, align_bytes=64)
+        nc.sync.dma_start(xw_table[:], x_words[0].rearrange("p n t -> p (n t)").bitcast(I32))
+        offs_list = load_list("offs_list", offs)
+        cand_list = load_list("cand_list", cand)
+        for w, scales in enumerate((w1_scales, w2_scales)):
+            rows = scales[0].bitcast(I32)
+            for r in range(4):
+                nc.scalar.dma_start(ws_raw[r:P:32, w * H : (w + 1) * H].bitcast(I32), rows[r:16:4, :])
+        ww_raw = [keep.tile([P, 2 * H], U8, name=f"ww_raw{w}", align_bytes=64) for w in range(2)]
+        for w, words in enumerate((w1_words, w2_words)):
+            nc.gpsimd.dma_start(ww_raw[w][:].bitcast(I32), words[0].bitcast(I32))
+        n1_list = load_list("n1_list", n1)
+        n2_list = load_list("n2_list", n2)
+        n3_list = load_list("n3_list", n3)
+        n4_list = load_list("n4_list", n4)
+
+        ww = [keep.tile([P, 2 * H], U8, name=f"ww{w}", align_bytes=64) for w in range(2)]
+        ws = keep.tile([P, PACK, 2, P], U8, align_bytes=64)
+        for t in range(PACK):
+            for w in range(2):
+                nc.scalar.copy(
+                    ww[w][:].bitcast(U16)[:, P * t : P * (t + 1)],
+                    ww_raw[w][:].bitcast(U16)[:, t:H:PACK],
+                )
+            nc.gpsimd.tensor_copy(ws[:, t, :, :], ws_raw[:].rearrange("p (w m t) -> p t w m", w=2, t=PACK)[:, t, :, :])
+
+        hz_bytes = keep.tile([P, S], U8, align_bytes=64)
+        nc.vector.tensor_copy(hz_bytes[:], xs_table[:].indirect(hz_list[:]))
+        hz_scale = keep.tile([P, S], U8, align_bytes=64)
+        nc.vector.tensor_copy(hz_scale[:].bitcast(I32), hz_bytes[:].bitcast(I32))
+        for e in range(2):
+            nc.sync.dma_start(hz_scale[2 + e : P : 32, :].bitcast(I32), hz_bytes[16 + e : P : 32, :].bitcast(I32))
+        offs_scale = keep.tile([P, S], U8, align_bytes=64)
+        nc.vector.tensor_copy(offs_scale[:], xs_table[:].indirect(offs_list[:]))
+        cand_scale = keep.tile([P, C], U8, align_bytes=64)
+        nc.vector.tensor_copy(cand_scale[:].rearrange("p (t m) -> p m t", t=PACK), xs_table[:].indirect(cand_list[:]))
+
+        xw_u32 = xw_table[:].bitcast(U32)
+        picked = keep.tile([P, 3 * S], U32, tag="bytes_then_words", align_bytes=64)
+        offs_words, hz_words, cand_words = (picked[:, i * S : (i + 1) * S] for i in range(3))
+        nc.vector.tensor_copy(offs_words, xw_u32.indirect(offs_list[:]))
+        nc.vector.tensor_copy(hz_words, xw_u32.indirect(hz_list[:]))
+        nc.vector.tensor_copy(cand_words.rearrange("p (t m) -> p m t", t=PACK), xw_u32.indirect(cand_list[:]))
+
+        gs_rows = load_rows("gs_rows", gs, "hz_bytes")
+        sl_rows = load_rows("sl_rows", sl, "ww_raw0")
+        th_rows = load_rows("th_rows", th, "ww_raw1")
+        neg_sl = keep.tile([P, PACK], F32)
+        nc.gpsimd.tensor_scalar(neg_sl[:], sl_rows[:], -1.0, 0.0, ALU.mult, ALU.add)
+        bias_rows = keep.tile([P, PACK], F32)
+        nc.gpsimd.tensor_tensor(bias_rows[:], neg_sl[:], th_rows[:], ALU.mult)
+
+        y_sb = []
+        for t in range(PACK):
+            bank = psum.tile([P, S], F32, name=f"y_bank{t}")
+            for w, (words, scale) in enumerate(((offs_words, offs_scale), (hz_words, hz_scale))):
+                nc.tensor.matmul_mx(
+                    out=bank[:],
+                    lhsT=ww[w][:, 2 * P * t : 2 * P * (t + 1)].bitcast(FP4X4),
+                    lhsT_scale=ws[:, t, w, :],
+                    rhs=words.bitcast(FP8X4),
+                    rhs_scale=scale[:],
+                    start=(w == 0),
+                    stop=(w == 1),
+                )
+            y_t = keep.tile([P, S], F32, name=f"y{t}")
+            nc.scalar.copy(y_t[:], bank[:])
+            y_sb.append(y_t)
+
+        z_bf = [keep.tile([P, HALF, PACK], BF16, name=f"z_bf{h}", align_bytes=64) for h in range(2)]
+        for t in range(PACK):
+            ds = keep.tile([P, 2 * S], F32, name="ds", bufs=2)
+            ds2 = keep.tile([P, 2 * S], F32, name="ds2")
+            nc.vector.tensor_copy(ds[:].indirect(n1_list[:]), y_sb[t][:])
+            nc.vector.tensor_copy(ds2[:].indirect(n2_list[:]), y_sb[t][:])
+            top = keep.tile([P, S], F32, name="top")
+            if t < PACK - 1:
+                nc.vector.tensor_tensor(top[:], ds[:, :S], ds2[:, :S], ALU.max)
+                for h in range(2):
+                    cols = slice(h * HALF, (h + 1) * HALF)
+                    nc.scalar.activation(z_bf[h][:, :, t], top[:, cols], ACT.Copy, scale=gs_rows[:, t : t + 1])
+            else:
+                for h in range(2):
+                    cols = slice(h * HALF, (h + 1) * HALF)
+                    nc.vector.tensor_tensor(top[:, cols], ds[:, cols], ds2[:, cols], ALU.max)
+                for h in range(2):
+                    cols = slice(h * HALF, (h + 1) * HALF)
+                    nc.vector.tensor_scalar(z_bf[h][:, :, t], top[:, cols], gs_rows[:, t : t + 1], None, ALU.mult)
+
+        z_words = keep.tile([P, S], U32, align_bytes=64)
+        z_scale = keep.tile([P, S], U8, align_bytes=64)
+        s_bank = [psum.tile([P, S], F32, name=f"s_bank{t}") for t in range(PACK)]
+        for h in range(2):
+            cols = slice(h * HALF, (h + 1) * HALF)
+            nc.vector.quantize_mx(
+                out=z_words[:, cols].bitcast(FP8X4),
+                scales=z_scale[:, cols],
+                in_=z_bf[h][:].rearrange("p c t -> p (c t)"),
+            )
+            for t in range(PACK):
+                nc.tensor.matmul_mx(
+                    out=s_bank[t][:, cols],
+                    lhsT=cand_words[:, P * t : P * (t + 1)].bitcast(FP8X4),
+                    lhsT_scale=cand_scale[:, P * t : P * (t + 1)],
+                    rhs=z_words[:, cols].bitcast(FP8X4),
+                    rhs_scale=z_scale[:, cols],
+                    start=True,
+                    stop=True,
+                )
+
+        out_rows = out.rearrange("(p t) c -> t p c", t=PACK)
+        s_sb, st_sb = [], []
+
+        def score(t):
+            s_t = keep.tile([P, 2 * S], F32, name=f"s{t}")
+            nc.vector.tensor_scalar(s_t[:, :S], s_bank[t][:], 0.0625, None, ALU.mult)
+            s_sb.append(s_t)
+
+        def gate(t):
+            sg = keep.tile([P, S], F32, name=f"sg{t}")
+            nc.scalar.activation(
+                sg[:],
+                s_sb[t][:].indirect(n3_list[:]),
+                ACT.Sigmoid,
+                bias=bias_rows[:, t : t + 1],
+                scale=sl_rows[:, t : t + 1],
+            )
+            st = keep.tile([P, 2 * S], F32, name=f"st{t}")
+            nc.vector.tensor_tensor(st[:, :S], s_sb[t][:, :S], sg[:], ALU.mult)
+            st_sb.append(st)
+
+        def finish(t):
+            fetched = keep.tile([P, S], F32, name=f"fetched{t}")
+            result = keep.tile([P, S], F32, name=f"result{t}")
+            width = HALF if t == PACK - 1 else S
+            for c0 in range(0, S, width):
+                cols = slice(c0, c0 + width)
+                nc.scalar.activation(
+                    fetched[:, cols],
+                    st_sb[t][:].indirect(n4_list[:, c0 // 16 : (c0 + width) // 16]),
+                    ACT.Copy,
+                )
+                nc.vector.scalar_tensor_tensor(
+                    result[:, cols], fetched[:, cols], -0.5, st_sb[t][:, cols], ALU.mult, ALU.add
+                )
+                nc.sync.dma_start(out_rows[t, :, cols], result[:, cols])
+
+        for t in range(PACK):
+            score(t)
+        for t in range(PACK + 1):
+            if t < PACK:
+                gate(t)
+            if t >= 1:
+                finish(t - 1)

@@ -30,6 +30,13 @@ def tile_picked_thcsendtwoehp_none_p_kernel(
         keep = ctx.enter_context(tc.tile_pool(name="keep", bufs=1))
         psum = ctx.enter_context(tc.psum_pool(name="psum", bufs=1))
 
+        whole = slice(0, S)
+        halves = (slice(0, HALF), slice(HALF, S))
+        tapered = (slice(0, HALF), slice(HALF, S - P), slice(S - P, S))
+
+        def entries(list_tile, cols):
+            return list_tile[:, cols.start // 16 : cols.stop // 16]
+
         def load_list(name, src):
             tile = keep.tile([P, LIST_COLS], U16, name=name)
             nc.sync.dma_start(tile[:], src)
@@ -46,12 +53,9 @@ def tile_picked_thcsendtwoehp_none_p_kernel(
         nc.vector.memset(ws_raw[:].bitcast(I32), 0)
 
         hz_list = load_list("hz_list", hz)
-        xs_rows = x_scales[0].bitcast(I32)
-        for r in range(4):
-            part_step, row_step = (16, 2) if r < 2 else (32, 4)
-            nc.scalar.dma_start(xs_table[r:P:part_step, :].bitcast(I32), xs_rows[r:16:row_step, :])
+        nc.scalar.dma_start(xs_table[0:P:8, :].bitcast(I32), x_scales[0].bitcast(I32))
         xw_table = keep.tile([P, T], I32, align_bytes=64)
-        nc.sync.dma_start(xw_table[:], x_words[0].rearrange("p n t -> p (n t)").bitcast(I32))
+        nc.gpsimd.dma_start(xw_table[:], x_words[0].rearrange("p n t -> p (n t)").bitcast(I32))
         offs_list = load_list("offs_list", offs)
         cand_list = load_list("cand_list", cand)
         for w, scales in enumerate((w1_scales, w2_scales)):
@@ -76,80 +80,89 @@ def tile_picked_thcsendtwoehp_none_p_kernel(
                 )
             nc.gpsimd.tensor_copy(ws[:, t, :, :], ws_raw[:].rearrange("p (w m t) -> p t w m", w=2, t=PACK)[:, t, :, :])
 
-        hz_bytes = keep.tile([P, S], U8, align_bytes=64)
-        nc.vector.tensor_copy(hz_bytes[:], xs_table[:].indirect(hz_list[:]))
-        hz_scale = keep.tile([P, S], U8, align_bytes=64)
-        nc.vector.tensor_copy(hz_scale[:].bitcast(I32), hz_bytes[:].bitcast(I32))
-        for e in range(2):
-            nc.sync.dma_start(hz_scale[2 + e : P : 32, :].bitcast(I32), hz_bytes[16 + e : P : 32, :].bitcast(I32))
-        offs_scale = keep.tile([P, S], U8, align_bytes=64)
-        nc.vector.tensor_copy(offs_scale[:], xs_table[:].indirect(offs_list[:]))
-        cand_scale = keep.tile([P, C], U8, align_bytes=64)
-        nc.vector.tensor_copy(cand_scale[:].rearrange("p (t m) -> p m t", t=PACK), xs_table[:].indirect(cand_list[:]))
+        def place_scale_rows(name, gathered):
+            placed = keep.tile(gathered.shape, U8, name=name, align_bytes=64)
+            nc.vector.tensor_copy(placed[:].bitcast(I32), gathered[:].bitcast(I32))
+            for r in range(1, 4):
+                nc.sync.dma_start(placed[r:P:32, :].bitcast(I32), gathered[8 * r : P : 32, :].bitcast(I32))
+            return placed
+
+        token_bytes = keep.tile([P, 2 * S], U8, align_bytes=64)
+        nc.vector.tensor_copy(token_bytes[:, :S], xs_table[:].indirect(offs_list[:]))
+        nc.vector.tensor_copy(token_bytes[:, S:], xs_table[:].indirect(hz_list[:]))
+        token_scale = place_scale_rows("token_scale", token_bytes)
+        offs_scale, hz_scale = token_scale[:, :S], token_scale[:, S:]
+        cand_bytes = keep.tile([P, C], U8, align_bytes=64)
+        nc.vector.tensor_copy(cand_bytes[:].rearrange("p (t m) -> p m t", t=PACK), xs_table[:].indirect(cand_list[:]))
+        cand_scale = place_scale_rows("cand_scale", cand_bytes)
 
         xw_u32 = xw_table[:].bitcast(U32)
         picked = keep.tile([P, 3 * S], U32, tag="bytes_then_words", align_bytes=64)
         offs_words, hz_words, cand_words = (picked[:, i * S : (i + 1) * S] for i in range(3))
         nc.vector.tensor_copy(offs_words, xw_u32.indirect(offs_list[:]))
-        nc.vector.tensor_copy(hz_words, xw_u32.indirect(hz_list[:]))
+        for cols in halves:
+            nc.vector.tensor_copy(hz_words[:, cols], xw_u32.indirect(entries(hz_list, cols)))
         nc.vector.tensor_copy(cand_words.rearrange("p (t m) -> p m t", t=PACK), xw_u32.indirect(cand_list[:]))
 
-        gs_rows = load_rows("gs_rows", gs, "hz_bytes")
-        sl_rows = load_rows("sl_rows", sl, "ww_raw0")
-        th_rows = load_rows("th_rows", th, "ww_raw1")
+        gs_rows = load_rows("gs_rows", gs, "cand_bytes")
+
+        y_sb = []
+        for t in range(PACK):
+            y_t = keep.tile([P, S], F32, name=f"y{t}")
+            for cols in halves if t == 0 else (whole,):
+                tag = "y_bank" if cols.stop == S else "y_bank_first"
+                bank = psum.tile([P, cols.stop - cols.start], F32, name="bank", tag=tag)
+                for w, (words, scale) in enumerate(((offs_words, offs_scale), (hz_words, hz_scale))):
+                    nc.tensor.matmul_mx(
+                        out=bank[:],
+                        lhsT=ww[w][:, 2 * P * t : 2 * P * (t + 1)].bitcast(FP4X4),
+                        lhsT_scale=ws[:, t, w, :],
+                        rhs=words[:, cols].bitcast(FP8X4),
+                        rhs_scale=scale[:, cols],
+                        start=(w == 0),
+                        stop=(w == 1),
+                    )
+                nc.scalar.copy(y_t[:, cols], bank[:])
+            y_sb.append(y_t)
+
+        sl_rows = load_rows("sl_rows", sl, "token_scale")
+        th_rows = load_rows("th_rows", th, "ws")
         neg_sl = keep.tile([P, PACK], F32)
         nc.gpsimd.tensor_scalar(neg_sl[:], sl_rows[:], -1.0, 0.0, ALU.mult, ALU.add)
         bias_rows = keep.tile([P, PACK], F32)
         nc.gpsimd.tensor_tensor(bias_rows[:], neg_sl[:], th_rows[:], ALU.mult)
 
-        y_sb = []
-        for t in range(PACK):
-            bank = psum.tile([P, S], F32, name=f"y_bank{t}")
-            for w, (words, scale) in enumerate(((offs_words, offs_scale), (hz_words, hz_scale))):
-                nc.tensor.matmul_mx(
-                    out=bank[:],
-                    lhsT=ww[w][:, 2 * P * t : 2 * P * (t + 1)].bitcast(FP4X4),
-                    lhsT_scale=ws[:, t, w, :],
-                    rhs=words.bitcast(FP8X4),
-                    rhs_scale=scale[:],
-                    start=(w == 0),
-                    stop=(w == 1),
-                )
-            y_t = keep.tile([P, S], F32, name=f"y{t}")
-            nc.scalar.copy(y_t[:], bank[:])
-            y_sb.append(y_t)
-
         z_bf = [keep.tile([P, HALF, PACK], BF16, name=f"z_bf{h}", align_bytes=64) for h in range(2)]
         for t in range(PACK):
             ds = keep.tile([P, 2 * S], F32, name="ds", bufs=2)
             ds2 = keep.tile([P, 2 * S], F32, name="ds2")
-            nc.vector.tensor_copy(ds[:].indirect(n1_list[:]), y_sb[t][:])
+            for cols in halves if t == 0 else (whole,):
+                nc.vector.tensor_copy(ds[:].indirect(entries(n1_list, cols)), y_sb[t][:, cols])
             nc.vector.tensor_copy(ds2[:].indirect(n2_list[:]), y_sb[t][:])
             top = keep.tile([P, S], F32, name="top")
+            gs_t = gs_rows[:, t : t + 1]
             if t < PACK - 1:
-                nc.vector.tensor_tensor(top[:], ds[:, :S], ds2[:, :S], ALU.max)
-                for h in range(2):
-                    cols = slice(h * HALF, (h + 1) * HALF)
-                    nc.scalar.activation(z_bf[h][:, :, t], top[:, cols], ACT.Copy, scale=gs_rows[:, t : t + 1])
+                nc.vector.tensor_tensor(top[:], ds[:, whole], ds2[:, whole], ALU.max)
+                for h, cols in enumerate(halves):
+                    nc.scalar.activation(z_bf[h][:, :, t], top[:, cols], ACT.Copy, scale=gs_t)
             else:
-                for h in range(2):
-                    cols = slice(h * HALF, (h + 1) * HALF)
-                    nc.vector.tensor_tensor(top[:, cols], ds[:, cols], ds2[:, cols], ALU.max)
-                for h in range(2):
-                    cols = slice(h * HALF, (h + 1) * HALF)
-                    nc.vector.tensor_scalar(z_bf[h][:, :, t], top[:, cols], gs_rows[:, t : t + 1], None, ALU.mult)
+                first, second = halves
+                nc.vector.tensor_tensor(top[:, second], ds[:, second], ds2[:, second], ALU.max)
+                nc.scalar.activation(z_bf[1][:, :, t], top[:, second], ACT.Copy, scale=gs_t)
+                nc.vector.tensor_tensor(top[:, first], ds[:, first], ds2[:, first], ALU.max)
+                nc.vector.tensor_scalar(z_bf[0][:, :, t], top[:, first], gs_t, None, ALU.mult)
 
         z_words = keep.tile([P, S], U32, align_bytes=64)
         z_scale = keep.tile([P, S], U8, align_bytes=64)
-        s_bank = [psum.tile([P, S], F32, name=f"s_bank{t}") for t in range(PACK)]
-        for h in range(2):
-            cols = slice(h * HALF, (h + 1) * HALF)
+        for h, cols in enumerate(halves):
             nc.vector.quantize_mx(
                 out=z_words[:, cols].bitcast(FP8X4),
                 scales=z_scale[:, cols],
                 in_=z_bf[h][:].rearrange("p c t -> p (c t)"),
             )
-            for t in range(PACK):
+        s_bank = [psum.tile([P, S], F32, name=f"s_bank{t}") for t in range(PACK)]
+        for t in range(PACK):
+            for cols in halves if t == 0 else (whole,):
                 nc.tensor.matmul_mx(
                     out=s_bank[t][:, cols],
                     lhsT=cand_words[:, P * t : P * (t + 1)].bitcast(FP8X4),
@@ -165,7 +178,12 @@ def tile_picked_thcsendtwoehp_none_p_kernel(
 
         def score(t):
             s_t = keep.tile([P, 2 * S], F32, name=f"s{t}")
-            nc.vector.tensor_scalar(s_t[:, :S], s_bank[t][:], 0.0625, None, ALU.mult)
+            if t == 0:
+                for h in range(2):
+                    cols = slice(h * HALF, (h + 1) * HALF)
+                    nc.scalar.activation(s_t[:, cols], s_bank[t][:, cols], ACT.Copy, scale=0.0625)
+            else:
+                nc.vector.tensor_scalar(s_t[:, :S], s_bank[t][:], 0.0625, None, ALU.mult)
             s_sb.append(s_t)
 
         def gate(t):
@@ -177,19 +195,17 @@ def tile_picked_thcsendtwoehp_none_p_kernel(
                 bias=bias_rows[:, t : t + 1],
                 scale=sl_rows[:, t : t + 1],
             )
-            st = keep.tile([P, 2 * S], F32, name=f"st{t}")
+            st = keep.tile([P, S if t == PACK - 1 else 2 * S], F32, name=f"st{t}")
             nc.vector.tensor_tensor(st[:, :S], s_sb[t][:, :S], sg[:], ALU.mult)
             st_sb.append(st)
 
         def finish(t):
             fetched = keep.tile([P, S], F32, name=f"fetched{t}")
             result = keep.tile([P, S], F32, name=f"result{t}")
-            width = HALF if t == PACK - 1 else S
-            for c0 in range(0, S, width):
-                cols = slice(c0, c0 + width)
+            for cols in tapered if t == PACK - 1 else (whole,):
                 nc.scalar.activation(
                     fetched[:, cols],
-                    st_sb[t][:].indirect(n4_list[:, c0 // 16 : (c0 + width) // 16]),
+                    st_sb[t][:].indirect(entries(n4_list, cols)),
                     ACT.Copy,
                 )
                 nc.vector.scalar_tensor_tensor(

@@ -47,10 +47,18 @@ def tile_picked_thcsendtwoehp_none_p_kernel(
             nc.sync.dma_start(tile[:], src.rearrange("(p t) o -> p (t o)", t=PACK))
             return tile
 
-        xs_table = keep.tile([P, T], U8, tag="bytes_then_words", align_bytes=64)
+        warm_in = keep.tile([P, 1], F32)
+        warm_out = keep.tile([P, 1], F32)
+        nc.vector.memset(warm_in[:], 0.0)
+        nc.scalar.activation(warm_out[:], warm_in[:], ACT.Sigmoid)
+        xs_table = keep.tile([P, T], U8, align_bytes=64)
         ws_raw = keep.tile([P, 2 * H], U8, align_bytes=64)
         nc.gpsimd.memset(xs_table[:].bitcast(I32), 0)
         nc.vector.memset(ws_raw[:].bitcast(I32), 0)
+        token_scale = keep.tile([P, 2 * S], U8, align_bytes=64)
+        cand_scale = keep.tile([P, C], U8, align_bytes=64)
+        nc.vector.memset(token_scale[:].bitcast(I32), 0)
+        nc.vector.memset(cand_scale[:].bitcast(I32), 0)
 
         hz_list = load_list("hz_list", hz)
         nc.scalar.dma_start(xs_table[0:P:8, :].bitcast(I32), x_scales[0].bitcast(I32))
@@ -61,7 +69,7 @@ def tile_picked_thcsendtwoehp_none_p_kernel(
         for w, scales in enumerate((w1_scales, w2_scales)):
             rows = scales[0].bitcast(I32)
             for r in range(4):
-                nc.scalar.dma_start(ws_raw[r:P:32, w * H : (w + 1) * H].bitcast(I32), rows[r:16:4, :])
+                nc.sync.dma_start(ws_raw[r:P:32, w * H : (w + 1) * H].bitcast(I32), rows[r:16:4, :])
         ww_raw = [keep.tile([P, 2 * H], U8, name=f"ww_raw{w}", align_bytes=64) for w in range(2)]
         for w, words in enumerate((w1_words, w2_words)):
             nc.gpsimd.dma_start(ww_raw[w][:].bitcast(I32), words[0].bitcast(I32))
@@ -80,29 +88,27 @@ def tile_picked_thcsendtwoehp_none_p_kernel(
                 )
             nc.gpsimd.tensor_copy(ws[:, t, :, :], ws_raw[:].rearrange("p (w m t) -> p t w m", w=2, t=PACK)[:, t, :, :])
 
-        def place_scale_rows(name, gathered):
-            placed = keep.tile(gathered.shape, U8, name=name, align_bytes=64)
-            nc.vector.tensor_copy(placed[:].bitcast(I32), gathered[:].bitcast(I32))
-            for r in range(1, 4):
+        def place_scale_rows(placed, gathered):
+            for r in range(4):
                 nc.sync.dma_start(placed[r:P:32, :].bitcast(I32), gathered[8 * r : P : 32, :].bitcast(I32))
-            return placed
 
         token_bytes = keep.tile([P, 2 * S], U8, align_bytes=64)
         nc.vector.tensor_copy(token_bytes[:, :S], xs_table[:].indirect(offs_list[:]))
         nc.vector.tensor_copy(token_bytes[:, S:], xs_table[:].indirect(hz_list[:]))
-        token_scale = place_scale_rows("token_scale", token_bytes)
+        place_scale_rows(token_scale, token_bytes)
         offs_scale, hz_scale = token_scale[:, :S], token_scale[:, S:]
         cand_bytes = keep.tile([P, C], U8, align_bytes=64)
         nc.vector.tensor_copy(cand_bytes[:].rearrange("p (t m) -> p m t", t=PACK), xs_table[:].indirect(cand_list[:]))
-        cand_scale = place_scale_rows("cand_scale", cand_bytes)
+        place_scale_rows(cand_scale, cand_bytes)
 
         xw_u32 = xw_table[:].bitcast(U32)
-        picked = keep.tile([P, 3 * S], U32, tag="bytes_then_words", align_bytes=64)
-        offs_words, hz_words, cand_words = (picked[:, i * S : (i + 1) * S] for i in range(3))
-        nc.vector.tensor_copy(offs_words, xw_u32.indirect(offs_list[:]))
+        hz_words = keep.tile([P, S], U32, align_bytes=64)
+        offs_words = keep.tile([P, S], U32, align_bytes=64)
+        cand_words = keep.tile([P, C], U32, align_bytes=64)
+        nc.vector.tensor_copy(hz_words[:], xw_u32.indirect(hz_list[:]))
         for cols in halves:
-            nc.vector.tensor_copy(hz_words[:, cols], xw_u32.indirect(entries(hz_list, cols)))
-        nc.vector.tensor_copy(cand_words.rearrange("p (t m) -> p m t", t=PACK), xw_u32.indirect(cand_list[:]))
+            nc.vector.tensor_copy(offs_words[:, cols], xw_u32.indirect(entries(offs_list, cols)))
+        nc.vector.tensor_copy(cand_words[:].rearrange("p (t m) -> p m t", t=PACK), xw_u32.indirect(cand_list[:]))
 
         gs_rows = load_rows("gs_rows", gs, "cand_bytes")
 
@@ -110,17 +116,17 @@ def tile_picked_thcsendtwoehp_none_p_kernel(
         for t in range(PACK):
             y_t = keep.tile([P, S], F32, name=f"y{t}")
             for cols in halves if t == 0 else (whole,):
-                tag = "y_bank" if cols.stop == S else "y_bank_first"
+                tag = f"bank{t}" if cols.stop == S else "bank_first"
                 bank = psum.tile([P, cols.stop - cols.start], F32, name="bank", tag=tag)
-                for w, (words, scale) in enumerate(((offs_words, offs_scale), (hz_words, hz_scale))):
+                for w, words, scale in ((1, hz_words, hz_scale), (0, offs_words, offs_scale)):
                     nc.tensor.matmul_mx(
                         out=bank[:],
                         lhsT=ww[w][:, 2 * P * t : 2 * P * (t + 1)].bitcast(FP4X4),
                         lhsT_scale=ws[:, t, w, :],
                         rhs=words[:, cols].bitcast(FP8X4),
                         rhs_scale=scale[:, cols],
-                        start=(w == 0),
-                        stop=(w == 1),
+                        start=(w == 1),
+                        stop=(w == 0),
                     )
                 nc.scalar.copy(y_t[:, cols], bank[:])
             y_sb.append(y_t)
@@ -133,36 +139,53 @@ def tile_picked_thcsendtwoehp_none_p_kernel(
         nc.gpsimd.tensor_tensor(bias_rows[:], neg_sl[:], th_rows[:], ALU.mult)
 
         z_bf = [keep.tile([P, HALF, PACK], BF16, name=f"z_bf{h}", align_bytes=64) for h in range(2)]
-        for t in range(PACK):
-            ds = keep.tile([P, 2 * S], F32, name="ds", bufs=2)
-            ds2 = keep.tile([P, 2 * S], F32, name="ds2")
-            for cols in halves if t == 0 else (whole,):
-                nc.vector.tensor_copy(ds[:].indirect(entries(n1_list, cols)), y_sb[t][:, cols])
-            nc.vector.tensor_copy(ds2[:].indirect(n2_list[:]), y_sb[t][:])
-            top = keep.tile([P, S], F32, name="top")
+        first, second = halves
+        quarters = (slice(0, P), slice(P, HALF))
+        ds, ds2 = {}, {}
+
+        def send_n1(t, cols):
+            if cols.start == 0:
+                ds[t] = keep.tile([P, 2 * S], F32, name="ds", bufs=2)
+            nc.vector.tensor_copy(ds[t][:].indirect(entries(n1_list, cols)), y_sb[t][:, cols])
+
+        def send_n2(t):
+            ds2[t] = keep.tile([P, 2 * S], F32, name="ds2", bufs=2)
+            nc.vector.tensor_copy(ds2[t][:].indirect(n2_list[:]), y_sb[t][:])
+
+        def weigh(t):
+            top = keep.tile([P, S], F32, name="top", tag=f"top{min(t, PACK - 2)}")
             gs_t = gs_rows[:, t : t + 1]
             if t < PACK - 1:
-                nc.vector.tensor_tensor(top[:], ds[:, whole], ds2[:, whole], ALU.max)
+                nc.vector.tensor_tensor(top[:], ds[t][:, whole], ds2[t][:, whole], ALU.max)
                 for h, cols in enumerate(halves):
                     nc.scalar.activation(z_bf[h][:, :, t], top[:, cols], ACT.Copy, scale=gs_t)
             else:
-                first, second = halves
-                nc.vector.tensor_tensor(top[:, second], ds[:, second], ds2[:, second], ALU.max)
+                nc.vector.tensor_tensor(top[:, second], ds[t][:, second], ds2[t][:, second], ALU.max)
                 nc.scalar.activation(z_bf[1][:, :, t], top[:, second], ACT.Copy, scale=gs_t)
-                nc.vector.tensor_tensor(top[:, first], ds[:, first], ds2[:, first], ALU.max)
-                nc.vector.tensor_scalar(z_bf[0][:, :, t], top[:, first], gs_t, None, ALU.mult)
+                for cols in quarters:
+                    nc.vector.tensor_tensor(top[:, cols], ds[t][:, cols], ds2[t][:, cols], ALU.max)
+                for cols in quarters:
+                    nc.vector.tensor_scalar(z_bf[0][:, cols, t], top[:, cols], gs_t, None, ALU.mult)
+
+        for t in range(PACK):
+            for cols in halves if t == 0 else (whole,):
+                send_n1(t, cols)
+            if t > 0:
+                weigh(t - 1)
+            send_n2(t)
+        weigh(PACK - 1)
 
         z_words = keep.tile([P, S], U32, align_bytes=64)
         z_scale = keep.tile([P, S], U8, align_bytes=64)
-        for h, cols in enumerate(halves):
+        for h, cols in ((1, second), (0, first)):
             nc.vector.quantize_mx(
                 out=z_words[:, cols].bitcast(FP8X4),
                 scales=z_scale[:, cols],
                 in_=z_bf[h][:].rearrange("p c t -> p (c t)"),
             )
-        s_bank = [psum.tile([P, S], F32, name=f"s_bank{t}") for t in range(PACK)]
+        s_bank = [psum.tile([P, S], F32, name="s_bank", tag=f"bank{t}") for t in range(PACK)]
         for t in range(PACK):
-            for cols in halves if t == 0 else (whole,):
+            for cols in (second, first) if t == 0 else (whole,):
                 nc.tensor.matmul_mx(
                     out=s_bank[t][:, cols],
                     lhsT=cand_words[:, P * t : P * (t + 1)].bitcast(FP8X4),
@@ -179,8 +202,7 @@ def tile_picked_thcsendtwoehp_none_p_kernel(
         def score(t):
             s_t = keep.tile([P, 2 * S], F32, name=f"s{t}")
             if t == 0:
-                for h in range(2):
-                    cols = slice(h * HALF, (h + 1) * HALF)
+                for cols in (second, first):
                     nc.scalar.activation(s_t[:, cols], s_bank[t][:, cols], ACT.Copy, scale=0.0625)
             else:
                 nc.vector.tensor_scalar(s_t[:, :S], s_bank[t][:], 0.0625, None, ALU.mult)

@@ -177,24 +177,34 @@ def tile_picked_thcsendtwoehp_none_p_kernel(
 
         z_words = keep.tile([P, S], U32, align_bytes=64)
         z_scale = keep.tile([P, S], U8, align_bytes=64)
-        for h, cols in ((1, second), (0, first)):
+        z_pieces = (second,) + quarters
+        for cols in z_pieces:
+            h = cols.start // HALF
+            local = slice(cols.start - h * HALF, cols.stop - h * HALF)
             nc.vector.quantize_mx(
                 out=z_words[:, cols].bitcast(FP8X4),
                 scales=z_scale[:, cols],
-                in_=z_bf[h][:].rearrange("p c t -> p (c t)"),
+                in_=z_bf[h][:, local, :].rearrange("p c t -> p (c t)"),
             )
+
+        def product(bank, t, cols):
+            nc.tensor.matmul_mx(
+                out=bank,
+                lhsT=cand_words[:, P * t : P * (t + 1)].bitcast(FP8X4),
+                lhsT_scale=cand_scale[:, P * t : P * (t + 1)],
+                rhs=z_words[:, cols].bitcast(FP8X4),
+                rhs_scale=z_scale[:, cols],
+                start=True,
+                stop=True,
+            )
+
         s_bank = [psum.tile([P, S], F32, name="s_bank", tag=f"bank{t}") for t in range(PACK)]
-        for t in range(PACK):
-            for cols in (second, first) if t == 0 else (whole,):
-                nc.tensor.matmul_mx(
-                    out=s_bank[t][:, cols],
-                    lhsT=cand_words[:, P * t : P * (t + 1)].bitcast(FP8X4),
-                    lhsT_scale=cand_scale[:, P * t : P * (t + 1)],
-                    rhs=z_words[:, cols].bitcast(FP8X4),
-                    rhs_scale=z_scale[:, cols],
-                    start=True,
-                    stop=True,
-                )
+        s_last = psum.tile([P, P], F32, name="s_last", tag="bank_first")
+        product(s_bank[0][:, second], 0, second)
+        product(s_bank[0][:, quarters[0]], 0, quarters[0])
+        product(s_last[:], 0, quarters[1])
+        for t in range(1, PACK):
+            product(s_bank[t][:], t, whole)
 
         out_rows = out.rearrange("(p t) c -> t p c", t=PACK)
         s_sb, st_sb = [], []
@@ -202,8 +212,9 @@ def tile_picked_thcsendtwoehp_none_p_kernel(
         def score(t):
             s_t = keep.tile([P, 2 * S], F32, name=f"s{t}")
             if t == 0:
-                for cols in (second, first):
+                for cols in (second, quarters[0]):
                     nc.scalar.activation(s_t[:, cols], s_bank[t][:, cols], ACT.Copy, scale=0.0625)
+                nc.vector.tensor_scalar(s_t[:, quarters[1]], s_last[:], 0.0625, None, ALU.mult)
             else:
                 nc.vector.tensor_scalar(s_t[:, :S], s_bank[t][:], 0.0625, None, ALU.mult)
             s_sb.append(s_t)

from contextlib import ExitStack

import concourse.mybir as mybir

K, T, S, H, C = 512, 2048, 512, 512, 512
FLOPS = 3 * 2 * K * H * S

F32 = mybir.dt.float32
BF16 = mybir.dt.bfloat16
I32 = mybir.dt.int32
U32 = mybir.dt.uint32
U16 = mybir.dt.uint16
U8 = mybir.dt.uint8
FP8X4 = mybir.dt.float8_e4m3fn_x4
FP4X4 = mybir.dt.float4_e2m1fn_x4
ALU = mybir.AluOpType
ACT = mybir.ActivationFunctionType

P = 128
PACK = 4
HALF = S // 2
LIST_COLS = S // 16


def tile_picked_thcsendtwoehp_none_p_kernel(
    tc, x_words, x_scales, w1_words, w1_scales, w2_words, w2_scales, gs, sl, th, offs, hz, n1, n2, cand, n3, n4, out
):
    nc = tc.nc
    with ExitStack() as ctx:
        keep = ctx.enter_context(tc.tile_pool(name="keep", bufs=1))
        psum = ctx.enter_context(tc.psum_pool(name="psum", bufs=1))

        whole = slice(0, S)
        halves = (slice(0, HALF), slice(HALF, S))
        tapered = (slice(0, HALF), slice(HALF, S - P), slice(S - P, S))

        def entries(list_tile, cols):
            return list_tile[:, cols.start // 16 : cols.stop // 16]

        def load_list(name, src):
            tile = keep.tile([P, LIST_COLS], U16, name=name)
            nc.sync.dma_start(tile[:], src)
            return tile

        def load_rows(name, src, tag):
            tile = keep.tile([P, PACK], F32, name=name, tag=tag, align_bytes=64)
            nc.sync.dma_start(tile[:], src.rearrange("(p t) o -> p (t o)", t=PACK))
            return tile

        warm_in = keep.tile([P, 1], F32)
        warm_out = keep.tile([P, 1], F32)
        nc.vector.memset(warm_in[:], 0.0)
        nc.scalar.activation(warm_out[:], warm_in[:], ACT.Sigmoid)
        xs_table = keep.tile([P, T], U8, align_bytes=64)
        ws_raw = keep.tile([P, 2 * H], U8, align_bytes=64)
        nc.gpsimd.memset(xs_table[:].bitcast(I32), 0)
        nc.vector.memset(ws_raw[:].bitcast(I32), 0)
        token_scale = keep.tile([P, 2 * S], U8, align_bytes=64)
        cand_scale = keep.tile([P, C], U8, align_bytes=64)
        nc.vector.memset(token_scale[:].bitcast(I32), 0)
        nc.vector.memset(cand_scale[:].bitcast(I32), 0)

        hz_list = load_list("hz_list", hz)
        nc.scalar.dma_start(xs_table[0:P:8, :].bitcast(I32), x_scales[0].bitcast(I32))
        xw_table = keep.tile([P, T], I32, align_bytes=64)
        nc.gpsimd.dma_start(xw_table[:], x_words[0].rearrange("p n t -> p (n t)").bitcast(I32))
        offs_list = load_list("offs_list", offs)
        cand_list = load_list("cand_list", cand)
        for w, scales in enumerate((w1_scales, w2_scales)):
            rows = scales[0].bitcast(I32)
            for r in range(4):
                nc.sync.dma_start(ws_raw[r:P:32, w * H : (w + 1) * H].bitcast(I32), rows[r:16:4, :])
        ww_raw = [keep.tile([P, 2 * H], U8, name=f"ww_raw{w}", align_bytes=64) for w in range(2)]
        for w, words in enumerate((w1_words, w2_words)):
            nc.gpsimd.dma_start(ww_raw[w][:].bitcast(I32), words[0].bitcast(I32))
        n1_list = load_list("n1_list", n1)
        n2_list = load_list("n2_list", n2)
        n3_list = load_list("n3_list", n3)
        n4_list = load_list("n4_list", n4)

        ww = [keep.tile([P, 2 * H], U8, name=f"ww{w}", align_bytes=64) for w in range(2)]
        ws = keep.tile([P, PACK, 2, P], U8, align_bytes=64)
        for t in range(PACK):
            for w in range(2):
                nc.scalar.copy(
                    ww[w][:].bitcast(U16)[:, P * t : P * (t + 1)],
                    ww_raw[w][:].bitcast(U16)[:, t:H:PACK],
                )
            nc.gpsimd.tensor_copy(ws[:, t, :, :], ws_raw[:].rearrange("p (w m t) -> p t w m", w=2, t=PACK)[:, t, :, :])

        def place_scale_rows(placed, gathered):
            for r in range(4):
                nc.sync.dma_start(placed[r:P:32, :].bitcast(I32), gathered[8 * r : P : 32, :].bitcast(I32))

        token_bytes = keep.tile([P, 2 * S], U8, align_bytes=64)
        nc.vector.tensor_copy(token_bytes[:, :S], xs_table[:].indirect(offs_list[:]))
        nc.vector.tensor_copy(token_bytes[:, S:], xs_table[:].indirect(hz_list[:]))
        place_scale_rows(token_scale, token_bytes)
        offs_scale, hz_scale = token_scale[:, :S], token_scale[:, S:]
        cand_bytes = keep.tile([P, C], U8, align_bytes=64)
        nc.vector.tensor_copy(cand_bytes[:].rearrange("p (t m) -> p m t", t=PACK), xs_table[:].indirect(cand_list[:]))
        place_scale_rows(cand_scale, cand_bytes)

        xw_u32 = xw_table[:].bitcast(U32)
        hz_words = keep.tile([P, S], U32, align_bytes=64)
        offs_words = keep.tile([P, S], U32, align_bytes=64)
        cand_words = keep.tile([P, C], U32, align_bytes=64)
        nc.vector.tensor_copy(hz_words[:], xw_u32.indirect(hz_list[:]))
        for cols in halves:
            nc.vector.tensor_copy(offs_words[:, cols], xw_u32.indirect(entries(offs_list, cols)))
        nc.vector.tensor_copy(cand_words[:].rearrange("p (t m) -> p m t", t=PACK), xw_u32.indirect(cand_list[:]))

        gs_rows = load_rows("gs_rows", gs, "cand_bytes")

        y_sb = []
        for t in range(PACK):
            y_t = keep.tile([P, S], F32, name=f"y{t}")
            for cols in halves if t == 0 else (whole,):
                tag = f"bank{t}" if cols.stop == S else "bank_first"
                bank = psum.tile([P, cols.stop - cols.start], F32, name="bank", tag=tag)
                for w, words, scale in ((1, hz_words, hz_scale), (0, offs_words, offs_scale)):
                    nc.tensor.matmul_mx(
                        out=bank[:],
                        lhsT=ww[w][:, 2 * P * t : 2 * P * (t + 1)].bitcast(FP4X4),
                        lhsT_scale=ws[:, t, w, :],
                        rhs=words[:, cols].bitcast(FP8X4),
                        rhs_scale=scale[:, cols],
                        start=(w == 1),
                        stop=(w == 0),
                    )
                nc.scalar.copy(y_t[:, cols], bank[:])
            y_sb.append(y_t)

        sl_rows = load_rows("sl_rows", sl, "token_scale")
        th_rows = load_rows("th_rows", th, "ws")
        neg_sl = keep.tile([P, PACK], F32)
        nc.gpsimd.tensor_scalar(neg_sl[:], sl_rows[:], -1.0, 0.0, ALU.mult, ALU.add)
        bias_rows = keep.tile([P, PACK], F32)
        nc.gpsimd.tensor_tensor(bias_rows[:], neg_sl[:], th_rows[:], ALU.mult)

        z_bf = [keep.tile([P, HALF, PACK], BF16, name=f"z_bf{h}", align_bytes=64) for h in range(2)]
        first, second = halves
        quarters = (slice(0, P), slice(P, HALF))
        ds, ds2 = {}, {}

        def send_n1(t, cols):
            if cols.start == 0:
                ds[t] = keep.tile([P, 2 * S], F32, name="ds", bufs=2)
            nc.vector.tensor_copy(ds[t][:].indirect(entries(n1_list, cols)), y_sb[t][:, cols])

        def send_n2(t):
            ds2[t] = keep.tile([P, 2 * S], F32, name="ds2", bufs=2)
            nc.vector.tensor_copy(ds2[t][:].indirect(n2_list[:]), y_sb[t][:])

        def weigh(t):
            top = keep.tile([P, S], F32, name="top", tag=f"top{min(t, PACK - 2)}")
            gs_t = gs_rows[:, t : t + 1]
            if t < PACK - 1:
                nc.vector.tensor_tensor(top[:], ds[t][:, whole], ds2[t][:, whole], ALU.max)
                for h, cols in enumerate(halves):
                    nc.scalar.activation(z_bf[h][:, :, t], top[:, cols], ACT.Copy, scale=gs_t)
            else:
                nc.vector.tensor_tensor(top[:, second], ds[t][:, second], ds2[t][:, second], ALU.max)
                nc.scalar.activation(z_bf[1][:, :, t], top[:, second], ACT.Copy, scale=gs_t)
                for cols in quarters:
                    nc.vector.tensor_tensor(top[:, cols], ds[t][:, cols], ds2[t][:, cols], ALU.max)
                for cols in quarters:
                    nc.vector.tensor_scalar(z_bf[0][:, cols, t], top[:, cols], gs_t, None, ALU.mult)

        for t in range(PACK):
            for cols in halves if t == 0 else (whole,):
                send_n1(t, cols)
            if t > 0:
                weigh(t - 1)
            send_n2(t)
        weigh(PACK - 1)

        z_words = keep.tile([P, S], U32, align_bytes=64)
        z_scale = keep.tile([P, S], U8, align_bytes=64)
        z_pieces = (second,) + quarters
        for cols in z_pieces:
            h = cols.start // HALF
            local = slice(cols.start - h * HALF, cols.stop - h * HALF)
            nc.vector.quantize_mx(
                out=z_words[:, cols].bitcast(FP8X4),
                scales=z_scale[:, cols],
                in_=z_bf[h][:, local, :].rearrange("p c t -> p (c t)"),
            )

        def product(bank, t, cols):
            nc.tensor.matmul_mx(
                out=bank,
                lhsT=cand_words[:, P * t : P * (t + 1)].bitcast(FP8X4),
                lhsT_scale=cand_scale[:, P * t : P * (t + 1)],
                rhs=z_words[:, cols].bitcast(FP8X4),
                rhs_scale=z_scale[:, cols],
                start=True,
                stop=True,
            )

        s_bank = [psum.tile([P, S], F32, name="s_bank", tag=f"bank{t}") for t in range(PACK)]
        s_last = psum.tile([P, P], F32, name="s_last", tag="bank_first")
        product(s_bank[0][:, second], 0, second)
        product(s_bank[0][:, quarters[0]], 0, quarters[0])
        product(s_last[:], 0, quarters[1])
        for t in range(1, PACK):
            product(s_bank[t][:], t, whole)

        out_rows = out.rearrange("(p t) c -> t p c", t=PACK)
        s_sb, st_sb = [], []

        def score(t):
            s_t = keep.tile([P, 2 * S], F32, name=f"s{t}")
            if t == 0:
                for cols in (second, quarters[0]):
                    nc.scalar.activation(s_t[:, cols], s_bank[t][:, cols], ACT.Copy, scale=0.0625)
                nc.vector.tensor_scalar(s_t[:, quarters[1]], s_last[:], 0.0625, None, ALU.mult)
            else:
                nc.vector.tensor_scalar(s_t[:, :S], s_bank[t][:], 0.0625, None, ALU.mult)
            s_sb.append(s_t)

        def gate(t):
            sg = keep.tile([P, S], F32, name=f"sg{t}")
            nc.scalar.activation(
                sg[:],
                s_sb[t][:].indirect(n3_list[:]),
                ACT.Sigmoid,
                bias=bias_rows[:, t : t + 1],
                scale=sl_rows[:, t : t + 1],
            )
            st = keep.tile([P, S if t == PACK - 1 else 2 * S], F32, name=f"st{t}")
            nc.vector.tensor_tensor(st[:, :S], s_sb[t][:, :S], sg[:], ALU.mult)
            st_sb.append(st)

        def finish(t):
            fetched = keep.tile([P, S], F32, name=f"fetched{t}")
            result = keep.tile([P, S], F32, name=f"result{t}")
            for cols in tapered if t == PACK - 1 else (whole,):
                nc.scalar.activation(
                    fetched[:, cols],
                    st_sb[t][:].indirect(entries(n4_list, cols)),
                    ACT.Copy,
                )
                nc.vector.scalar_tensor_tensor(
                    result[:, cols], fetched[:, cols], -0.5, st_sb[t][:, cols], ALU.mult, ALU.add
                )
                nc.sync.dma_start(out_rows[t, :, cols], result[:, cols])

        for t in range(PACK):
            score(t)
        for t in range(PACK + 1):
            if t < PACK:
                gate(t)
            if t >= 1:
                finish(t - 1)
